import numpy as np
import ml_dtypes


def mxq(x, axis, fmt="e4m3"):
    dtype, down = {"e4m3": (ml_dtypes.float8_e4m3fn, 7), "e5m2": (ml_dtypes.float8_e5m2, 14)}[fmt]
    v = np.moveaxis(np.asarray(x, np.float32).astype(ml_dtypes.bfloat16).astype(np.float64), axis, -1)
    blocks = v.reshape(v.shape[:-1] + (-1, 32))
    amax = np.abs(blocks).max(-1, keepdims=True)
    byte = np.maximum(np.where(amax > 0, np.frexp(amax)[1] - 1 + 127, 0) - down, 1)
    scale = np.exp2(byte - 127.0)
    codes = (blocks / scale).astype(np.float32).astype(dtype).astype(np.float64)
    return np.moveaxis((codes * scale).reshape(v.shape), -1, axis)


WIDE = False


def mx_kscale(k):
    if not WIDE:
        return np.ones(k)
    levels = np.array([10, -10, 5, -5, 0])
    if k % 512:
        return np.exp2(np.random.permutation(np.resize(levels, k // 32))).repeat(32)
    a = np.empty((k // 512, 16))
    for p in range(k // 512):
        a[p, :8] = np.random.permutation(np.resize(levels, 8))
        for g in range(8):
            far = levels[np.abs(levels - a[p, g]) >= 10]
            a[p, g + 8] = far[np.random.randint(len(far))]
    return np.exp2(a.ravel()).repeat(32)


def f64(x):
    return np.asarray(x).astype(np.float64)


def striped(idx):
    return np.tile(idx.reshape(-1, 16).T, (8, 1)).astype(np.uint16)


def unstriped(offs):
    return offs[:16].T.reshape(-1).astype(np.int64)


E2M1 = np.array([0.0, 0.5, 1.0, 1.5, 2.0, 3.0, 4.0, 6.0, -0.0, -0.5, -1.0, -1.5, -2.0, -3.0, -4.0, -6.0])


def pack_weight(w, fmt):
    k, n = w.shape
    w = f64(np.asarray(w, np.float32).astype(ml_dtypes.bfloat16)).reshape(k // 32, 32, n)
    amax = np.abs(w).max(1)
    if fmt == "e4m3":
        byte = np.frexp(amax)[1] - 1 + 127 - 7
    else:
        mant, ex = np.frexp(amax / 6.0)
        byte = np.where(mant > 0.5, ex, ex - 1) + 127
    byte = np.clip(np.where(amax > 0, byte, 1), 1, 254)
    scaled = (w * np.exp2(127.0 - byte)[:, None, :]).reshape(k, n).astype(np.float32)
    by_word = np.ascontiguousarray(scaled.reshape(k // 512, 128, 4, n).transpose(0, 1, 3, 2))
    if fmt == "e4m3":
        words = by_word.astype(ml_dtypes.float8_e4m3fn).view(np.uint8)
    else:
        c = by_word.astype(ml_dtypes.float4_e2m1fn).view(np.uint8) & 0xF
        words = (c[..., 0::2] | (c[..., 1::2] << 4)).reshape(k // 512, 128, 2 * n)
    return np.ascontiguousarray(words), np.ascontiguousarray(byte.astype(np.uint8).reshape(k // 512, 16, n))


def unpack_weight(words, scales, fmt):
    g, _, n = scales.shape
    words = np.ascontiguousarray(words).reshape(g, 128, n, -1)
    if fmt == "e4m3":
        vals = words.view(ml_dtypes.float8_e4m3fn).astype(np.float64)
    else:
        nib = np.empty((g, 128, n, 4), np.uint8)
        nib[..., 0::2] = words & 0xF
        nib[..., 1::2] = words >> 4
        vals = E2M1[nib]
    vals = vals * np.repeat(np.exp2(scales.astype(np.float64) - 127.0), 8, axis=1)[..., None]
    return vals.transpose(0, 1, 3, 2).reshape(g * 512, n)


def gelu(v):
    return 0.5 * v * (1.0 + np.tanh(np.sqrt(2.0 / np.pi) * (v + 0.044715 * v**3)))


K, K2, T, S, P, H, N, T2 = 1024, 512, 2048, 1024, 512, 512, 384, 2048

def setup_inputs():
    n = np.random.standard_normal
    s, s2, u = mx_kscale(K)[:, None], mx_kscale(K2)[:, None], mx_kscale(H)[:, None]
    tab_words, tab_scales = pack_weight(n((K, T)) * s, "e4m3")
    tab2_words, tab2_scales = pack_weight(n((K2, T)) * s2, "e4m3")
    wm_words, wm_scales = pack_weight(1.5 * n((K, N)) / np.sqrt(K) / s, "e2m1")
    wy2_words, wy2_scales = pack_weight(n((H, N)) / np.sqrt(H) / u, "e4m3")
    perm = np.random.permutation(T2)
    return {
        "tab_words": tab_words, "tab_scales": tab_scales,
        "tab2_words": tab2_words, "tab2_scales": tab2_scales,
        "offs": striped(np.random.permutation(T)[:S]),
        "offs2": striped(np.random.permutation(T)[:P]),
        "pos1": striped(np.random.permutation(S)[:P]),
        "offs3": striped(perm[:S]), "offs4": striped(perm[S:S + P]),
        "w1": (0.52 * n((K, H)) / np.sqrt(K) / s).astype(np.float32),
        "w2": (1.5 * n((K2, H)) / np.sqrt(K2) / s2 * u.T).astype(np.float32),
        "wm_words": wm_words, "wm_scales": wm_scales,
        "gain": (2.0 * np.exp(0.3 * n(H)) * u[:, 0]).astype(np.float32),
        "vec": (0.7 * n(H) * u[:, 0]).astype(np.float32),
        "wy1": (1.2 * n((H, N)) / np.sqrt(H) / u).astype(np.float32),
        "wy2_words": wy2_words, "wy2_scales": wy2_scales,
        "page1": n((N, T2)).astype(np.float32),
        "wg1": np.exp(0.3 * n((128, S))).astype(np.float32),
        "wg2": np.exp(0.3 * n((128, P))).astype(np.float32)}

def reference(tab_words, tab_scales, tab2_words, tab2_scales, offs, offs2, pos1, offs3, offs4, w1, w2, wm_words, wm_scales, gain, vec, wy1, wy2_words, wy2_scales, page1, wg1, wg2):
    v = unpack_weight(tab_words, tab_scales, "e4m3")[:, unstriped(offs)]
    v2 = unpack_weight(tab2_words, tab2_scales, "e4m3")[:, unstriped(offs2)]
    h1 = mxq(f64(w1), 0, "e4m3").T @ v
    side = unpack_weight(wm_words, wm_scales, "e2m1").T @ v
    h2 = mxq(f64(w2), 0, "e4m3").T @ v2
    z1 = f64(gain)[:, None] * np.sin(h1)
    z2 = h2 * h1[:, unstriped(pos1)] + f64(vec)[:, None]
    y1 = (mxq(f64(wy1), 0, "e4m3").T @ mxq(z1, 0, "e4m3")) + np.tanh(side)
    y2 = unpack_weight(wy2_words, wy2_scales, "e4m3").T @ mxq(z2, 0, "e4m3")
    out = f64(page1).copy()
    out[:, unstriped(offs3)] = np.tile(f64(wg1), (N // 128, 1)) * y1
    out[:, unstriped(offs4)] = np.tile(f64(wg2), (N // 128, 1)) * y2
    return out

@@ -1,0 +1,291 @@
+import math
+from contextlib import ExitStack
+
+import concourse.mybir as mybir
+
+K, K2, T, S, P, H, N, T2 = 1024, 512, 2048, 1024, 512, 512, 384, 2048
+FLOPS = 2 * (K * H * S + K * N * S + K2 * H * P + H * N * S + H * N * P)
+
+F32 = mybir.dt.float32
+BF16 = mybir.dt.bfloat16
+I32 = mybir.dt.int32
+U32 = mybir.dt.uint32
+U16 = mybir.dt.uint16
+U8 = mybir.dt.uint8
+FP8X4 = mybir.dt.float8_e4m3fn_x4
+FP4X4 = mybir.dt.float4_e2m1fn_x4
+ALU = mybir.AluOpType
+ACT = mybir.ActivationFunctionType
+
+PART = 128
+PACK = 4
+BANK = 512
+TURN = 2.0 * math.pi
+
+
+def tile_list_cargo_diversion_features_kernel(
+    tc, tab_words, tab_scales, tab2_words, tab2_scales, offs, offs2, pos1, offs3, offs4, w1, w2,
+    wm_words, wm_scales, gain, vec, wy1, wy2_words, wy2_scales, page1, wg1, wg2, out,
+):
+    nc = tc.nc
+    halves = S // BANK
+    pages = N // PART
+    with ExitStack() as ctx:
+        keep = ctx.enter_context(tc.tile_pool(name="keep", bufs=1))
+        ring = ctx.enter_context(tc.tile_pool(name="ring", bufs=2))
+        ring4 = ctx.enter_context(tc.tile_pool(name="ring4", bufs=4))
+        psum = ctx.enter_context(tc.psum_pool(name="psum", bufs=8))
+
+        def held(name, shape, dtype):
+            return keep.tile(shape, dtype, name=name, align_bytes=64)
+
+        def bank():
+            return psum.tile([PART, BANK], F32, name="bank")
+
+        def load_list(name, src):
+            tile = held(name, list(src.shape), U16)
+            nc.sync.dma_start(tile[:], src)
+            return tile
+
+        def words_of(packed):
+            return packed.rearrange("p n t -> p (n t)").bitcast(I32)
+
+        offs_sb = load_list("offs_sb", offs)
+        tab_plane = held("tab_plane", [PART, T], U8)
+        tab2_plane = held("tab2_plane", [PART, T], U8)
+        wm_plane = held("wm_plane", [PART, 2, N], U8)
+        wy2_plane = held("wy2_plane", [PART, N], U8)
+        v_plane1 = held("v_plane1", [PART, S], U8)
+        for plane in (tab_plane, tab2_plane, wy2_plane, wm_plane, v_plane1):
+            nc.vector.memset(plane[:].bitcast(I32), 0)
+
+        def quadrant(plane, q, rows):
+            return plane[32 * q : 32 * q + rows].bitcast(I32)
+
+        tab_sb = [held("tab_sb%d" % a, [PART, T], U32) for a in range(2)]
+        w1_raw = [ring.tile([PART, PACK, H], F32, name="w1_raw", tag="wide") for a in range(2)]
+        tab2_sb = held("tab2_sb", [PART, T], U32)
+        w2_raw = held("w2_raw", [PART, PACK, H], F32)
+        wm_sb = held("wm_sb", [PART, 2, 2 * N], U8)
+        wy2_sb = held("wy2_sb", [PART, N], U32)
+        wy1_raw = held("wy1_raw", [PART, PACK, N], F32)
+        gain_sb = held("gain_sb", [PART, PACK], F32)
+        vec_sb = held("vec_sb", [PART, PACK], F32)
+        wg1_sb = held("wg1_sb", [PART, S], F32)
+        wg2_sb = held("wg2_sb", [PART, P], F32)
+        page_sb = [held("page_sb%d" % i, [PART, T2], F32) for i in range(pages)]
+
+        def by_rows(weight):
+            return weight.rearrange("(p j) c -> p j c", j=PACK)
+
+        for q in range(4):
+            nc.sync.dma_start(quadrant(tab_plane, q, 8), tab_scales[:, 4 * q : 4 * q + 4, :].bitcast(I32))
+        nc.sync.dma_start(w1_raw[0][:], by_rows(w1[0:512, :]))
+        nc.sync.dma_start(tab_sb[0][:].bitcast(I32), words_of(tab_words[0]))
+        offs2_sb = load_list("offs2_sb", offs2)
+        for q in range(4):
+            nc.sync.dma_start(quadrant(tab2_plane, q, 4), tab2_scales[0, 4 * q : 4 * q + 4, :].bitcast(I32))
+        nc.sync.dma_start(w1_raw[1][:], by_rows(w1[512:1024, :]))
+        nc.sync.dma_start(tab_sb[1][:].bitcast(I32), words_of(tab_words[1]))
+        nc.sync.dma_start(w2_raw[:], by_rows(w2))
+        nc.sync.dma_start(tab2_sb[:].bitcast(I32), words_of(tab2_words[0]))
+        pos1_sb = load_list("pos1_sb", pos1)
+        nc.sync.dma_start(wm_sb[:].bitcast(I32), wm_words.rearrange("a p c -> p a c").bitcast(I32))
+        for q in range(4):
+            nc.sync.dma_start(
+                quadrant(wm_plane, q, 4), wm_scales[:, 4 * q : 4 * q + 4, :].rearrange("a r c -> r a c").bitcast(I32)
+            )
+        nc.sync.dma_start(vec_sb[:], vec.rearrange("(p t) -> p t", t=PACK))
+        nc.sync.dma_start(wy1_raw[:], by_rows(wy1))
+        nc.sync.dma_start(wy2_sb[:].bitcast(I32), words_of(wy2_words[0]))
+        for q in range(4):
+            nc.sync.dma_start(quadrant(wy2_plane, q, 4), wy2_scales[0, 4 * q : 4 * q + 4, :].bitcast(I32))
+        nc.sync.dma_start(page_sb[0][:], page1[0:PART, :])
+        offs4_sb = load_list("offs4_sb", offs4)
+        nc.sync.dma_start(wg2_sb[:], wg2)
+        nc.sync.dma_start(gain_sb[:], gain.rearrange("(p t) -> p t", t=PACK))
+        for i in range(1, pages):
+            nc.sync.dma_start(page_sb[i][:], page1[PART * i : PART * (i + 1), :])
+        offs3_sb = load_list("offs3_sb", offs3)
+        nc.sync.dma_start(wg1_sb[:], wg1)
+
+        def quantise(name, grouped, width):
+            codes = held(name + "_codes", [PART, width], U32)
+            plane = held(name + "_plane", [PART, width], U8)
+            nc.vector.quantize_mx(out=codes[:].bitcast(FP8X4), scales=plane[:], in_=grouped[:])
+            return codes, plane
+
+        def round_dealt(copy, name, raw):
+            grouped = held(name, [PART, PACK * H], BF16)
+            copy(
+                grouped[:].rearrange("p (t m j) -> p m j t", t=PACK, j=PACK),
+                raw[:].rearrange("p j (m t) -> p m j t", t=PACK),
+            )
+            return grouped
+
+        def interleave(name, rows, width):
+            grouped = held(name, [PART, PACK * width], BF16)
+            nc.scalar.copy(
+                grouped[:].rearrange("p (c i j) -> p c j i", i=PACK, j=PACK),
+                rows[:].rearrange("p j (c i) -> p c j i", i=PACK),
+            )
+            return grouped
+
+        def entries(lst, h):
+            return lst[:, h * (BANK // 16) : (h + 1) * (BANK // 16)]
+
+        def cols(i, width):
+            return slice(i * width, (i + 1) * width)
+
+        v_plane = held("v_plane", [PART, S], U8)
+        nc.vector.tensor_copy(v_plane[:], tab_plane[:].indirect(offs_sb[:]))
+        nc.gpsimd.dma_start(v_plane1[0:112, :].bitcast(I32), v_plane[4:116, :].bitcast(I32))
+        v_words = [[held("v_words%d%d" % (a, h), [PART, BANK], U32) for h in range(halves)] for a in range(2)]
+        h1_ps = [[bank() for t in range(PACK)] for h in range(halves)]
+        h1_sb = [held("h1_sb%d" % t, [PART, S], F32) for t in range(PACK)]
+        for a in range(2):
+            w1_codes, w1_plane = quantise("w1q%d" % a, round_dealt(nc.scalar.copy, "w1_bf%d" % a, w1_raw[a]), H)
+            for h in range(halves):
+                nc.vector.tensor_copy(v_words[a][h][:], tab_sb[a][:].indirect(entries(offs_sb, h)))
+                for t in range(PACK):
+                    nc.tensor.matmul_mx(
+                        out=h1_ps[h][t][:],
+                        lhsT=w1_codes[:, cols(t, PART)].bitcast(FP8X4),
+                        lhsT_scale=w1_plane[:, cols(t, PART)],
+                        rhs=v_words[a][h][:].bitcast(FP8X4),
+                        rhs_scale=v_plane[4 * a : PART, cols(h, BANK)],
+                        start=(a == 0),
+                        stop=(a == 1),
+                    )
+
+        def keep_h1(h, t):
+            nc.scalar.copy(h1_sb[t][:, cols(h, BANK)], h1_ps[h][t][:])
+
+        v2_plane = held("v2_plane", [PART, P], U8)
+        v2_words = held("v2_words", [PART, P], U32)
+        h2_sb = held("h2_sb", [PART, PACK, P], F32)
+        prod = held("prod", [PART, PACK, P], F32)
+        z2_rows = held("z2_rows", [PART, PACK, P], BF16)
+
+        def make_h2(t, w2q):
+            ps = bank()
+            nc.tensor.matmul_mx(
+                out=ps[:],
+                lhsT=w2q[0][:, cols(t, PART)].bitcast(FP8X4),
+                lhsT_scale=w2q[1][:, cols(t, PART)],
+                rhs=v2_words[:].bitcast(FP8X4),
+                rhs_scale=v2_plane[:],
+                start=True,
+                stop=True,
+            )
+            nc.scalar.copy(h2_sb[:, t, :], ps[:])
+
+        def make_z2(t):
+            nc.vector.tensor_tensor(prod[:, t, :], h1_sb[t][:].indirect(pos1_sb[:]), h2_sb[:, t, :], ALU.mult)
+            nc.scalar.activation(z2_rows[:, t, :], prod[:, t, :], ACT.Identity, bias=vec_sb[:, t : t + 1])
+
+        def place_y2(i, z2):
+            ps = bank()
+            nc.tensor.matmul_mx(
+                out=ps[:],
+                lhsT=wy2_sb[:, cols(i, PART)].bitcast(FP8X4),
+                lhsT_scale=wy2_plane[:, cols(i, PART)],
+                rhs=z2[0][:].bitcast(FP8X4),
+                rhs_scale=z2[1][:],
+                start=True,
+                stop=True,
+            )
+            y2 = ring4.tile([PART, P], F32, name="y2")
+            nc.scalar.copy(y2[:], ps[:])
+            nc.vector.tensor_tensor(page_sb[i][:].indirect(offs4_sb[:]), y2[:], wg2_sb[:], ALU.mult)
+
+        phase2 = [ring.tile([PART, 2, S], F32, name="phase2", tag="wide") for u in range(2)]
+        phase = [phase2[t // 2][:, t % 2, :] for t in range(PACK)]
+
+        def reduce_phase(t, turns):
+            nc.vector.tensor_scalar(turns, h1_sb[t][:], 1.0 / TURN, 1.0, ALU.mult, ALU.add)
+            nc.vector.scalar_tensor_tensor(phase[t], turns, -TURN, h1_sb[t][:], ALU.mult, ALU.add)
+
+        side_sb = [[held("side_sb%d%d" % (h, i), [PART, BANK], F32) for i in range(pages)] for h in range(halves)]
+
+        def make_side(h, i):
+            ps = bank()
+            for a in range(2):
+                nc.tensor.matmul_mx(
+                    out=ps[:],
+                    lhsT=wm_sb[:, a, cols(i, 2 * PART)].bitcast(FP4X4),
+                    lhsT_scale=wm_plane[:, a, cols(i, PART)],
+                    rhs=v_words[a][h][:].bitcast(FP8X4),
+                    rhs_scale=(v_plane, v_plane1)[a][:, cols(h, BANK)],
+                    start=(a == 0),
+                    stop=(a == 1),
+                )
+            nc.scalar.activation(side_sb[h][i][:], ps[:], ACT.Tanh)
+
+        z1_rows = [held("z1_rows%d" % h, [PART, PACK, BANK], BF16) for h in range(halves)]
+
+        def make_z1(h, t):
+            sine = z2_rows[:].rearrange("p t c -> p (t c)").bitcast(F32)[:, cols(t % 2, BANK)]
+            nc.scalar.activation(sine, phase[t][:, cols(h, BANK)], ACT.Sin, bias=TURN)
+            nc.scalar.activation(z1_rows[h][:, t, :], sine, ACT.Copy, scale=gain_sb[:, t : t + 1])
+
+        def place_y1(h, i, z1, y1=None):
+            ps = bank()
+            nc.tensor.matmul_mx(
+                out=ps[:],
+                lhsT=wy1_codes[:, cols(i, PART)].bitcast(FP8X4),
+                lhsT_scale=wy1_plane[:, cols(i, PART)],
+                rhs=z1[0][:].bitcast(FP8X4),
+                rhs_scale=z1[1][:],
+                start=True,
+                stop=True,
+            )
+            if y1 is None:
+                y1 = ring4.tile([PART, BANK], F32, name="y1")[:]
+            nc.vector.tensor_tensor(y1, ps[:], side_sb[h][i][:], ALU.add)
+            nc.vector.tensor_tensor(
+                page_sb[i][:].indirect(entries(offs3_sb, h)), y1, wg1_sb[:, cols(h, BANK)], ALU.mult
+            )
+
+        w2q = quantise("w2q", round_dealt(nc.vector.tensor_copy, "w2_bf", w2_raw), H)
+        nc.vector.tensor_copy(v2_plane[:], tab2_plane[:].indirect(offs2_sb[:]))
+        nc.vector.tensor_copy(v2_words[:], tab2_sb[:].indirect(offs2_sb[:]))
+        for h in range(halves):
+            for t in range(PACK):
+                keep_h1(h, t)
+        for t in range(PACK):
+            make_h2(t, w2q)
+        make_side(0, 0)
+        make_side(0, 1)
+        make_z2(0)
+        make_side(0, 2)
+        make_side(1, 0)
+        make_z2(1)
+        wy1_bf = interleave("wy1_bf", wy1_raw, N)
+        make_z2(2)
+        make_side(1, 1)
+        make_side(1, 2)
+        make_z2(3)
+        z2_bf = interleave("z2_bf", z2_rows, P)
+        z2 = quantise("z2q", z2_bf, P)
+        for i in range(pages):
+            place_y2(i, z2)
+        wy1_codes, wy1_plane = quantise("wy1q", wy1_bf, N)
+        reduce_phase(0, held("turns", [PART, S], I32)[:])
+        reduce_phase(1, h2_sb[:, 2:4, :].rearrange("p t c -> p (t c)").bitcast(I32))
+        reduce_phase(2, prod[:, 2:4, :].rearrange("p t c -> p (t c)").bitcast(I32))
+        reduce_phase(3, z2_bf[:].bitcast(I32))
+        for t in range(PACK):
+            make_z1(0, t)
+        z1a = quantise("z1q0", interleave("z1_bf0", z1_rows[0], BANK), BANK)
+        for t in range(PACK):
+            make_z1(1, t)
+        place_y1(0, 0, z1a)
+        place_y1(0, 1, z1a)
+        z1_last = interleave("z1_bf1", z1_rows[1], BANK)
+        z1b = quantise("z1q1", z1_last, BANK)
+        place_y1(0, 2, z1a, z1_last[:].bitcast(F32)[:, 0:BANK])
+        for i in range(pages):
+            place_y1(1, i, z1b)
+        for i in range(pages):
+            nc.sync.dma_start(out[PART * i : PART * (i + 1), :], page_sb[i][:])

@@ -78,9 +78,9 @@ def tile_list_cargo_diversion_features_kernel(
         def by_rows(weight):
             return weight.rearrange("(p j) c -> p j c", j=PACK)
 
+        nc.sync.dma_start(w1_raw[0][:], by_rows(w1[0:512, :]))
         for q in range(4):
             nc.sync.dma_start(quadrant(tab_plane, q, 8), tab_scales[:, 4 * q : 4 * q + 4, :].bitcast(I32))
-        nc.sync.dma_start(w1_raw[0][:], by_rows(w1[0:512, :]))
         nc.sync.dma_start(tab_sb[0][:].bitcast(I32), words_of(tab_words[0]))
         offs2_sb = load_list("offs2_sb", offs2)
         for q in range(4):
@@ -109,6 +109,10 @@ def tile_list_cargo_diversion_features_kernel(
         offs3_sb = load_list("offs3_sb", offs3)
         nc.sync.dma_start(wg1_sb[:], wg1)
 
+        warm = held("warm", [PART, 2], F32)
+        nc.vector.memset(warm[:, 0:1], 0.0)
+        nc.scalar.activation(warm[:, 1:2], warm[:, 0:1], ACT.Silu)
+
         def quantise(name, grouped, width):
             codes = held(name + "_codes", [PART, width], U32)
             plane = held(name + "_plane", [PART, width], U8)
@@ -123,8 +127,12 @@ def tile_list_cargo_diversion_features_kernel(
             )
             return grouped
 
-        def interleave(name, rows, width):
-            grouped = held(name, [PART, PACK * width], BF16)
+        def flat(tile):
+            return tile[:].rearrange("p t c -> p (t c)")
+
+        def interleave(name, rows, width, grouped=None):
+            if grouped is None:
+                grouped = held(name, [PART, PACK * width], BF16)
             nc.scalar.copy(
                 grouped[:].rearrange("p (c i j) -> p c j i", i=PACK, j=PACK),
                 rows[:].rearrange("p j (c i) -> p c j i", i=PACK),
@@ -184,7 +192,7 @@ def tile_list_cargo_diversion_features_kernel(
             nc.vector.tensor_tensor(prod[:, t, :], h1_sb[t][:].indirect(pos1_sb[:]), h2_sb[:, t, :], ALU.mult)
             nc.scalar.activation(z2_rows[:, t, :], prod[:, t, :], ACT.Identity, bias=vec_sb[:, t : t + 1])
 
-        def place_y2(i, z2):
+        def place_y2(i, z2, placed=None):
             ps = bank()
             nc.tensor.matmul_mx(
                 out=ps[:],
@@ -197,13 +205,16 @@ def tile_list_cargo_diversion_features_kernel(
             )
             y2 = ring4.tile([PART, P], F32, name="y2")
             nc.scalar.copy(y2[:], ps[:])
-            nc.vector.tensor_tensor(page_sb[i][:].indirect(offs4_sb[:]), y2[:], wg2_sb[:], ALU.mult)
+            if placed is None:
+                placed = ring4.tile([PART, BANK], F32, name="placed")[:]
+            nc.gpsimd.tensor_tensor(placed, y2[:], wg2_sb[:], ALU.mult)
+            nc.vector.tensor_copy(page_sb[i][:].indirect(offs4_sb[:]), placed)
 
         phase2 = [ring.tile([PART, 2, S], F32, name="phase2", tag="wide") for u in range(2)]
         phase = [phase2[t // 2][:, t % 2, :] for t in range(PACK)]
 
         def reduce_phase(t, turns):
-            nc.vector.tensor_scalar(turns, h1_sb[t][:], 1.0 / TURN, 1.0, ALU.mult, ALU.add)
+            nc.vector.tensor_scalar(turns, h1_sb[t][:], 1.0 / TURN, None, ALU.mult)
             nc.vector.scalar_tensor_tensor(phase[t], turns, -TURN, h1_sb[t][:], ALU.mult, ALU.add)
 
         side_sb = [[held("side_sb%d%d" % (h, i), [PART, BANK], F32) for i in range(pages)] for h in range(halves)]
@@ -226,10 +237,10 @@ def tile_list_cargo_diversion_features_kernel(
 
         def make_z1(h, t):
             sine = z2_rows[:].rearrange("p t c -> p (t c)").bitcast(F32)[:, cols(t % 2, BANK)]
-            nc.scalar.activation(sine, phase[t][:, cols(h, BANK)], ACT.Sin, bias=TURN)
+            nc.scalar.activation(sine, phase[t][:, cols(h, BANK)], ACT.Sin)
             nc.scalar.activation(z1_rows[h][:, t, :], sine, ACT.Copy, scale=gain_sb[:, t : t + 1])
 
-        def place_y1(h, i, z1, y1=None):
+        def place_y1(h, i, z1, placed=None):
             ps = bank()
             nc.tensor.matmul_mx(
                 out=ps[:],
@@ -240,12 +251,14 @@ def tile_list_cargo_diversion_features_kernel(
                 start=True,
                 stop=True,
             )
-            if y1 is None:
-                y1 = ring4.tile([PART, BANK], F32, name="y1")[:]
-            nc.vector.tensor_tensor(y1, ps[:], side_sb[h][i][:], ALU.add)
-            nc.vector.tensor_tensor(
-                page_sb[i][:].indirect(entries(offs3_sb, h)), y1, wg1_sb[:, cols(h, BANK)], ALU.mult
-            )
+            y1 = ring4.tile([PART, BANK], F32, name="y2")
+            nc.scalar.copy(y1[:], ps[:])
+            total = ring.tile([PART, BANK], F32, name="total", bufs=1)
+            nc.gpsimd.tensor_tensor(total[:], y1[:], side_sb[h][i][:], ALU.add)
+            if placed is None:
+                placed = ring4.tile([PART, BANK], F32, name="placed")[:]
+            nc.gpsimd.tensor_tensor(placed, total[:], wg1_sb[:, cols(h, BANK)], ALU.mult)
+            nc.vector.tensor_copy(page_sb[i][:].indirect(entries(offs3_sb, h)), placed)
 
         w2q = quantise("w2q", round_dealt(nc.vector.tensor_copy, "w2_bf", w2_raw), H)
         nc.vector.tensor_copy(v2_plane[:], tab2_plane[:].indirect(offs2_sb[:]))
@@ -255,21 +268,15 @@ def tile_list_cargo_diversion_features_kernel(
                 keep_h1(h, t)
         for t in range(PACK):
             make_h2(t, w2q)
-        make_side(0, 0)
-        make_side(0, 1)
-        make_z2(0)
-        make_side(0, 2)
-        make_side(1, 0)
-        make_z2(1)
-        wy1_bf = interleave("wy1_bf", wy1_raw, N)
-        make_z2(2)
-        make_side(1, 1)
-        make_side(1, 2)
-        make_z2(3)
+        for t in range(PACK):
+            make_z2(t)
+            if t < pages:
+                make_side(0, t)
         z2_bf = interleave("z2_bf", z2_rows, P)
         z2 = quantise("z2q", z2_bf, P)
-        for i in range(pages):
-            place_y2(i, z2)
+        wy1_bf = interleave(None, wy1_raw, N, flat(z2_rows)[:, 0 : PACK * N])
+        place_y2(0, z2)
+        place_y2(1, z2)
         wy1_codes, wy1_plane = quantise("wy1q", wy1_bf, N)
         reduce_phase(0, held("turns", [PART, S], I32)[:])
         reduce_phase(1, h2_sb[:, 2:4, :].rearrange("p t c -> p (t c)").bitcast(I32))
@@ -277,14 +284,18 @@ def tile_list_cargo_diversion_features_kernel(
         reduce_phase(3, z2_bf[:].bitcast(I32))
         for t in range(PACK):
             make_z1(0, t)
-        z1a = quantise("z1q0", interleave("z1_bf0", z1_rows[0], BANK), BANK)
+        z1_first = interleave("z1_bf0", z1_rows[0], BANK)
+        z1a = quantise("z1q0", z1_first, BANK)
+        place_y2(2, z2, flat(z1_rows[0]).bitcast(F32)[:, 0:BANK])
+        for i in range(pages):
+            make_side(1, i)
+        place_y1(0, 0, z1a)
         for t in range(PACK):
             make_z1(1, t)
-        place_y1(0, 0, z1a)
-        place_y1(0, 1, z1a)
         z1_last = interleave("z1_bf1", z1_rows[1], BANK)
         z1b = quantise("z1q1", z1_last, BANK)
-        place_y1(0, 2, z1a, z1_last[:].bitcast(F32)[:, 0:BANK])
+        place_y1(0, 1, z1a, flat(z1_rows[1]).bitcast(F32)[:, 0:BANK])
+        place_y1(0, 2, z1a)
         for i in range(pages):
             place_y1(1, i, z1b)
         for i in range(pages):

@@ -78,9 +78,9 @@ def tile_list_cargo_diversion_features_kernel(
         def by_rows(weight):
             return weight.rearrange("(p j) c -> p j c", j=PACK)
 
-        nc.sync.dma_start(w1_raw[0][:], by_rows(w1[0:512, :]))
         for q in range(4):
             nc.sync.dma_start(quadrant(tab_plane, q, 8), tab_scales[:, 4 * q : 4 * q + 4, :].bitcast(I32))
+        nc.sync.dma_start(w1_raw[0][:], by_rows(w1[0:512, :]))
         nc.sync.dma_start(tab_sb[0][:].bitcast(I32), words_of(tab_words[0]))
         offs2_sb = load_list("offs2_sb", offs2)
         for q in range(4):
@@ -109,9 +109,8 @@ def tile_list_cargo_diversion_features_kernel(
         offs3_sb = load_list("offs3_sb", offs3)
         nc.sync.dma_start(wg1_sb[:], wg1)
 
-        warm = held("warm", [PART, 2], F32)
-        nc.vector.memset(warm[:, 0:1], 0.0)
-        nc.scalar.activation(warm[:, 1:2], warm[:, 0:1], ACT.Silu)
+        warm = held("warm", [PART, 1], F32)
+        nc.scalar.activation(warm[:], w1_raw[0][:, 0, 0:1], ACT.Silu)
 
         def quantise(name, grouped, width):
             codes = held(name + "_codes", [PART, width], U32)
@@ -206,9 +205,10 @@ def tile_list_cargo_diversion_features_kernel(
             y2 = ring4.tile([PART, P], F32, name="y2")
             nc.scalar.copy(y2[:], ps[:])
             if placed is None:
-                placed = ring4.tile([PART, BANK], F32, name="placed")[:]
-            nc.gpsimd.tensor_tensor(placed, y2[:], wg2_sb[:], ALU.mult)
-            nc.vector.tensor_copy(page_sb[i][:].indirect(offs4_sb[:]), placed)
+                nc.vector.tensor_tensor(page_sb[i][:].indirect(offs4_sb[:]), y2[:], wg2_sb[:], ALU.mult)
+            else:
+                nc.gpsimd.tensor_tensor(placed, y2[:], wg2_sb[:], ALU.mult)
+                nc.vector.tensor_copy(page_sb[i][:].indirect(offs4_sb[:]), placed)
 
         phase2 = [ring.tile([PART, 2, S], F32, name="phase2", tag="wide") for u in range(2)]
         phase = [phase2[t // 2][:, t % 2, :] for t in range(PACK)]
@@ -217,7 +217,7 @@ def tile_list_cargo_diversion_features_kernel(
             nc.vector.tensor_scalar(turns, h1_sb[t][:], 1.0 / TURN, None, ALU.mult)
             nc.vector.scalar_tensor_tensor(phase[t], turns, -TURN, h1_sb[t][:], ALU.mult, ALU.add)
 
-        side_sb = [[held("side_sb%d%d" % (h, i), [PART, BANK], F32) for i in range(pages)] for h in range(halves)]
+        side_sb = [[held("side_sb%d" % i, [PART, BANK], F32)[:] for i in range(pages)], None]
 
         def make_side(h, i):
             ps = bank()
@@ -231,12 +231,12 @@ def tile_list_cargo_diversion_features_kernel(
                     start=(a == 0),
                     stop=(a == 1),
                 )
-            nc.scalar.activation(side_sb[h][i][:], ps[:], ACT.Tanh)
+            nc.scalar.activation(side_sb[h][i], ps[:], ACT.Tanh)
 
         z1_rows = [held("z1_rows%d" % h, [PART, PACK, BANK], BF16) for h in range(halves)]
 
         def make_z1(h, t):
-            sine = z2_rows[:].rearrange("p t c -> p (t c)").bitcast(F32)[:, cols(t % 2, BANK)]
+            sine = h2_sb[:, t % 2, :]
             nc.scalar.activation(sine, phase[t][:, cols(h, BANK)], ACT.Sin)
             nc.scalar.activation(z1_rows[h][:, t, :], sine, ACT.Copy, scale=gain_sb[:, t : t + 1])
 
@@ -254,7 +254,7 @@ def tile_list_cargo_diversion_features_kernel(
             y1 = ring4.tile([PART, BANK], F32, name="y2")
             nc.scalar.copy(y1[:], ps[:])
             total = ring.tile([PART, BANK], F32, name="total", bufs=1)
-            nc.gpsimd.tensor_tensor(total[:], y1[:], side_sb[h][i][:], ALU.add)
+            nc.gpsimd.tensor_tensor(total[:], y1[:], side_sb[h][i], ALU.add)
             if placed is None:
                 placed = ring4.tile([PART, BANK], F32, name="placed")[:]
             nc.gpsimd.tensor_tensor(placed, total[:], wg1_sb[:, cols(h, BANK)], ALU.mult)
@@ -275,9 +275,9 @@ def tile_list_cargo_diversion_features_kernel(
         z2_bf = interleave("z2_bf", z2_rows, P)
         z2 = quantise("z2q", z2_bf, P)
         wy1_bf = interleave(None, wy1_raw, N, flat(z2_rows)[:, 0 : PACK * N])
+        wy1_codes, wy1_plane = quantise("wy1q", wy1_bf, N)
         place_y2(0, z2)
         place_y2(1, z2)
-        wy1_codes, wy1_plane = quantise("wy1q", wy1_bf, N)
         reduce_phase(0, held("turns", [PART, S], I32)[:])
         reduce_phase(1, h2_sb[:, 2:4, :].rearrange("p t c -> p (t c)").bitcast(I32))
         reduce_phase(2, prod[:, 2:4, :].rearrange("p t c -> p (t c)").bitcast(I32))
@@ -287,8 +287,6 @@ def tile_list_cargo_diversion_features_kernel(
         z1_first = interleave("z1_bf0", z1_rows[0], BANK)
         z1a = quantise("z1q0", z1_first, BANK)
         place_y2(2, z2, flat(z1_rows[0]).bitcast(F32)[:, 0:BANK])
-        for i in range(pages):
-            make_side(1, i)
         place_y1(0, 0, z1a)
         for t in range(PACK):
             make_z1(1, t)
@@ -296,6 +294,9 @@ def tile_list_cargo_diversion_features_kernel(
         z1b = quantise("z1q1", z1_last, BANK)
         place_y1(0, 1, z1a, flat(z1_rows[1]).bitcast(F32)[:, 0:BANK])
         place_y1(0, 2, z1a)
+        side_sb[1] = [flat(z1_rows[0]).bitcast(F32)[:, BANK:S], z1_first[:].bitcast(F32)[:, 0:BANK], z1_first[:].bitcast(F32)[:, BANK:S]]
+        for i in range(pages):
+            make_side(1, i)
         for i in range(pages):
             place_y1(1, i, z1b)
         for i in range(pages):

import math
from contextlib import ExitStack

import concourse.mybir as mybir

K, K2, T, S, P, H, N, T2 = 1024, 512, 2048, 1024, 512, 512, 384, 2048
FLOPS = 2 * (K * H * S + K * N * S + K2 * H * P + H * N * S + H * N * P)

F32 = mybir.dt.float32
BF16 = mybir.dt.bfloat16
I32 = mybir.dt.int32
U32 = mybir.dt.uint32
U16 = mybir.dt.uint16
U8 = mybir.dt.uint8
FP8X4 = mybir.dt.float8_e4m3fn_x4
FP4X4 = mybir.dt.float4_e2m1fn_x4
ALU = mybir.AluOpType
ACT = mybir.ActivationFunctionType

PART = 128
PACK = 4
BANK = 512
TURN = 2.0 * math.pi


def tile_list_cargo_diversion_features_kernel(
    tc, tab_words, tab_scales, tab2_words, tab2_scales, offs, offs2, pos1, offs3, offs4, w1, w2,
    wm_words, wm_scales, gain, vec, wy1, wy2_words, wy2_scales, page1, wg1, wg2, out,
):
    nc = tc.nc
    halves = S // BANK
    pages = N // PART
    with ExitStack() as ctx:
        keep = ctx.enter_context(tc.tile_pool(name="keep", bufs=1))
        ring = ctx.enter_context(tc.tile_pool(name="ring", bufs=2))
        ring4 = ctx.enter_context(tc.tile_pool(name="ring4", bufs=4))
        psum = ctx.enter_context(tc.psum_pool(name="psum", bufs=8))

        def held(name, shape, dtype):
            return keep.tile(shape, dtype, name=name, align_bytes=64)

        def bank():
            return psum.tile([PART, BANK], F32, name="bank")

        def load_list(name, src):
            tile = held(name, list(src.shape), U16)
            nc.sync.dma_start(tile[:], src)
            return tile

        def words_of(packed):
            return packed.rearrange("p n t -> p (n t)").bitcast(I32)

        offs_sb = load_list("offs_sb", offs)
        tab_plane = held("tab_plane", [PART, T], U8)
        tab2_plane = held("tab2_plane", [PART, T], U8)
        wm_plane = held("wm_plane", [PART, 2, N], U8)
        wy2_plane = held("wy2_plane", [PART, N], U8)
        v_plane1 = held("v_plane1", [PART, S], U8)
        for plane in (tab_plane, tab2_plane, wy2_plane, wm_plane, v_plane1):
            nc.vector.memset(plane[:].bitcast(I32), 0)

        def quadrant(plane, q, rows):
            return plane[32 * q : 32 * q + rows].bitcast(I32)

        tab_sb = [held("tab_sb%d" % a, [PART, T], U32) for a in range(2)]
        w1_raw = [ring.tile([PART, PACK, H], F32, name="w1_raw", tag="wide") for a in range(2)]
        tab2_sb = held("tab2_sb", [PART, T], U32)
        w2_raw = held("w2_raw", [PART, PACK, H], F32)
        wm_sb = held("wm_sb", [PART, 2, 2 * N], U8)
        wy2_sb = held("wy2_sb", [PART, N], U32)
        wy1_raw = held("wy1_raw", [PART, PACK, N], F32)
        gain_sb = held("gain_sb", [PART, PACK], F32)
        vec_sb = held("vec_sb", [PART, PACK], F32)
        wg1_sb = held("wg1_sb", [PART, S], F32)
        wg2_sb = held("wg2_sb", [PART, P], F32)
        page_sb = [held("page_sb%d" % i, [PART, T2], F32) for i in range(pages)]

        def by_rows(weight):
            return weight.rearrange("(p j) c -> p j c", j=PACK)

        for q in range(4):
            nc.sync.dma_start(quadrant(tab_plane, q, 8), tab_scales[:, 4 * q : 4 * q + 4, :].bitcast(I32))
        nc.sync.dma_start(w1_raw[0][:], by_rows(w1[0:512, :]))
        nc.sync.dma_start(tab_sb[0][:].bitcast(I32), words_of(tab_words[0]))
        offs2_sb = load_list("offs2_sb", offs2)
        for q in range(4):
            nc.sync.dma_start(quadrant(tab2_plane, q, 4), tab2_scales[0, 4 * q : 4 * q + 4, :].bitcast(I32))
        nc.sync.dma_start(w1_raw[1][:], by_rows(w1[512:1024, :]))
        nc.sync.dma_start(tab_sb[1][:].bitcast(I32), words_of(tab_words[1]))
        nc.sync.dma_start(w2_raw[:], by_rows(w2))
        nc.sync.dma_start(tab2_sb[:].bitcast(I32), words_of(tab2_words[0]))
        pos1_sb = load_list("pos1_sb", pos1)
        nc.sync.dma_start(wm_sb[:].bitcast(I32), wm_words.rearrange("a p c -> p a c").bitcast(I32))
        for q in range(4):
            nc.sync.dma_start(
                quadrant(wm_plane, q, 4), wm_scales[:, 4 * q : 4 * q + 4, :].rearrange("a r c -> r a c").bitcast(I32)
            )
        nc.sync.dma_start(vec_sb[:], vec.rearrange("(p t) -> p t", t=PACK))
        nc.sync.dma_start(wy1_raw[:], by_rows(wy1))
        nc.sync.dma_start(wy2_sb[:].bitcast(I32), words_of(wy2_words[0]))
        for q in range(4):
            nc.sync.dma_start(quadrant(wy2_plane, q, 4), wy2_scales[0, 4 * q : 4 * q + 4, :].bitcast(I32))
        nc.sync.dma_start(page_sb[0][:], page1[0:PART, :])
        offs4_sb = load_list("offs4_sb", offs4)
        nc.sync.dma_start(wg2_sb[:], wg2)
        nc.sync.dma_start(gain_sb[:], gain.rearrange("(p t) -> p t", t=PACK))
        for i in range(1, pages):
            nc.sync.dma_start(page_sb[i][:], page1[PART * i : PART * (i + 1), :])
        offs3_sb = load_list("offs3_sb", offs3)
        nc.sync.dma_start(wg1_sb[:], wg1)

        warm = held("warm", [PART, 1], F32)
        nc.scalar.activation(warm[:], w1_raw[0][:, 0, 0:1], ACT.Silu)

        def quantise(name, grouped, width):
            codes = held(name + "_codes", [PART, width], U32)
            plane = held(name + "_plane", [PART, width], U8)
            nc.vector.quantize_mx(out=codes[:].bitcast(FP8X4), scales=plane[:], in_=grouped[:])
            return codes, plane

        def round_dealt(copy, name, raw):
            grouped = held(name, [PART, PACK * H], BF16)
            copy(
                grouped[:].rearrange("p (t m j) -> p m j t", t=PACK, j=PACK),
                raw[:].rearrange("p j (m t) -> p m j t", t=PACK),
            )
            return grouped

        def flat(tile):
            return tile[:].rearrange("p t c -> p (t c)")

        def interleave(name, rows, width, grouped=None):
            if grouped is None:
                grouped = held(name, [PART, PACK * width], BF16)
            nc.scalar.copy(
                grouped[:].rearrange("p (c i j) -> p c j i", i=PACK, j=PACK),
                rows[:].rearrange("p j (c i) -> p c j i", i=PACK),
            )
            return grouped

        def entries(lst, h):
            return lst[:, h * (BANK // 16) : (h + 1) * (BANK // 16)]

        def cols(i, width):
            return slice(i * width, (i + 1) * width)

        v_plane = held("v_plane", [PART, S], U8)
        nc.vector.tensor_copy(v_plane[:], tab_plane[:].indirect(offs_sb[:]))
        nc.gpsimd.dma_start(v_plane1[0:112, :].bitcast(I32), v_plane[4:116, :].bitcast(I32))
        v_words = [[held("v_words%d%d" % (a, h), [PART, BANK], U32) for h in range(halves)] for a in range(2)]
        h1_ps = [[bank() for t in range(PACK)] for h in range(halves)]
        h1_sb = [held("h1_sb%d" % t, [PART, S], F32) for t in range(PACK)]
        for a in range(2):
            w1_codes, w1_plane = quantise("w1q%d" % a, round_dealt(nc.scalar.copy, "w1_bf%d" % a, w1_raw[a]), H)
            for h in range(halves):
                nc.vector.tensor_copy(v_words[a][h][:], tab_sb[a][:].indirect(entries(offs_sb, h)))
                for t in range(PACK):
                    nc.tensor.matmul_mx(
                        out=h1_ps[h][t][:],
                        lhsT=w1_codes[:, cols(t, PART)].bitcast(FP8X4),
                        lhsT_scale=w1_plane[:, cols(t, PART)],
                        rhs=v_words[a][h][:].bitcast(FP8X4),
                        rhs_scale=v_plane[4 * a : PART, cols(h, BANK)],
                        start=(a == 0),
                        stop=(a == 1),
                    )

        def keep_h1(h, t):
            nc.scalar.copy(h1_sb[t][:, cols(h, BANK)], h1_ps[h][t][:])

        v2_plane = held("v2_plane", [PART, P], U8)
        v2_words = held("v2_words", [PART, P], U32)
        h2_sb = held("h2_sb", [PART, PACK, P], F32)
        prod = held("prod", [PART, PACK, P], F32)
        z2_rows = held("z2_rows", [PART, PACK, P], BF16)

        def make_h2(t, w2q):
            ps = bank()
            nc.tensor.matmul_mx(
                out=ps[:],
                lhsT=w2q[0][:, cols(t, PART)].bitcast(FP8X4),
                lhsT_scale=w2q[1][:, cols(t, PART)],
                rhs=v2_words[:].bitcast(FP8X4),
                rhs_scale=v2_plane[:],
                start=True,
                stop=True,
            )
            nc.scalar.copy(h2_sb[:, t, :], ps[:])

        def make_z2(t):
            nc.vector.tensor_tensor(prod[:, t, :], h1_sb[t][:].indirect(pos1_sb[:]), h2_sb[:, t, :], ALU.mult)
            nc.scalar.activation(z2_rows[:, t, :], prod[:, t, :], ACT.Identity, bias=vec_sb[:, t : t + 1])

        def place_y2(i, z2, placed=None):
            ps = bank()
            nc.tensor.matmul_mx(
                out=ps[:],
                lhsT=wy2_sb[:, cols(i, PART)].bitcast(FP8X4),
                lhsT_scale=wy2_plane[:, cols(i, PART)],
                rhs=z2[0][:].bitcast(FP8X4),
                rhs_scale=z2[1][:],
                start=True,
                stop=True,
            )
            y2 = ring4.tile([PART, P], F32, name="y2")
            nc.scalar.copy(y2[:], ps[:])
            if placed is None:
                nc.vector.tensor_tensor(page_sb[i][:].indirect(offs4_sb[:]), y2[:], wg2_sb[:], ALU.mult)
            else:
                nc.gpsimd.tensor_tensor(placed, y2[:], wg2_sb[:], ALU.mult)
                nc.vector.tensor_copy(page_sb[i][:].indirect(offs4_sb[:]), placed)

        phase2 = [ring.tile([PART, 2, S], F32, name="phase2", tag="wide") for u in range(2)]
        phase = [phase2[t // 2][:, t % 2, :] for t in range(PACK)]

        def reduce_phase(t, turns):
            nc.vector.tensor_scalar(turns, h1_sb[t][:], 1.0 / TURN, None, ALU.mult)
            nc.vector.scalar_tensor_tensor(phase[t], turns, -TURN, h1_sb[t][:], ALU.mult, ALU.add)

        side_sb = [[held("side_sb%d" % i, [PART, BANK], F32)[:] for i in range(pages)], None]

        def make_side(h, i):
            ps = bank()
            for a in range(2):
                nc.tensor.matmul_mx(
                    out=ps[:],
                    lhsT=wm_sb[:, a, cols(i, 2 * PART)].bitcast(FP4X4),
                    lhsT_scale=wm_plane[:, a, cols(i, PART)],
                    rhs=v_words[a][h][:].bitcast(FP8X4),
                    rhs_scale=(v_plane, v_plane1)[a][:, cols(h, BANK)],
                    start=(a == 0),
                    stop=(a == 1),
                )
            nc.scalar.activation(side_sb[h][i], ps[:], ACT.Tanh)

        z1_rows = [held("z1_rows%d" % h, [PART, PACK, BANK], BF16) for h in range(halves)]

        def make_z1(h, t):
            sine = h2_sb[:, t % 2, :]
            nc.scalar.activation(sine, phase[t][:, cols(h, BANK)], ACT.Sin)
            nc.scalar.activation(z1_rows[h][:, t, :], sine, ACT.Copy, scale=gain_sb[:, t : t + 1])

        def place_y1(h, i, z1, placed=None):
            ps = bank()
            nc.tensor.matmul_mx(
                out=ps[:],
                lhsT=wy1_codes[:, cols(i, PART)].bitcast(FP8X4),
                lhsT_scale=wy1_plane[:, cols(i, PART)],
                rhs=z1[0][:].bitcast(FP8X4),
                rhs_scale=z1[1][:],
                start=True,
                stop=True,
            )
            y1 = ring4.tile([PART, BANK], F32, name="y2")
            nc.scalar.copy(y1[:], ps[:])
            total = ring.tile([PART, BANK], F32, name="total", bufs=1)
            nc.gpsimd.tensor_tensor(total[:], y1[:], side_sb[h][i], ALU.add)
            if placed is None:
                placed = ring4.tile([PART, BANK], F32, name="placed")[:]
            nc.gpsimd.tensor_tensor(placed, total[:], wg1_sb[:, cols(h, BANK)], ALU.mult)
            nc.vector.tensor_copy(page_sb[i][:].indirect(entries(offs3_sb, h)), placed)

        w2q = quantise("w2q", round_dealt(nc.vector.tensor_copy, "w2_bf", w2_raw), H)
        nc.vector.tensor_copy(v2_plane[:], tab2_plane[:].indirect(offs2_sb[:]))
        nc.vector.tensor_copy(v2_words[:], tab2_sb[:].indirect(offs2_sb[:]))
        for h in range(halves):
            for t in range(PACK):
                keep_h1(h, t)
        for t in range(PACK):
            make_h2(t, w2q)
        for t in range(PACK):
            make_z2(t)
            if t < pages:
                make_side(0, t)
        z2_bf = interleave("z2_bf", z2_rows, P)
        z2 = quantise("z2q", z2_bf, P)
        wy1_bf = interleave(None, wy1_raw, N, flat(z2_rows)[:, 0 : PACK * N])
        wy1_codes, wy1_plane = quantise("wy1q", wy1_bf, N)
        place_y2(0, z2)
        place_y2(1, z2)
        reduce_phase(0, held("turns", [PART, S], I32)[:])
        reduce_phase(1, h2_sb[:, 2:4, :].rearrange("p t c -> p (t c)").bitcast(I32))
        reduce_phase(2, prod[:, 2:4, :].rearrange("p t c -> p (t c)").bitcast(I32))
        reduce_phase(3, z2_bf[:].bitcast(I32))
        for t in range(PACK):
            make_z1(0, t)
        z1_first = interleave("z1_bf0", z1_rows[0], BANK)
        z1a = quantise("z1q0", z1_first, BANK)
        place_y2(2, z2, flat(z1_rows[0]).bitcast(F32)[:, 0:BANK])
        place_y1(0, 0, z1a)
        for t in range(PACK):
            make_z1(1, t)
        z1_last = interleave("z1_bf1", z1_rows[1], BANK)
        z1b = quantise("z1q1", z1_last, BANK)
        place_y1(0, 1, z1a, flat(z1_rows[1]).bitcast(F32)[:, 0:BANK])
        place_y1(0, 2, z1a)
        side_sb[1] = [flat(z1_rows[0]).bitcast(F32)[:, BANK:S], z1_first[:].bitcast(F32)[:, 0:BANK], z1_first[:].bitcast(F32)[:, BANK:S]]
        for i in range(pages):
            make_side(1, i)
        for i in range(pages):
            place_y1(1, i, z1b)
        for i in range(pages):
            nc.sync.dma_start(out[PART * i : PART * (i + 1), :], page_sb[i][:])
